import numpy as np
import ml_dtypes


def mxq(x, axis, fmt="e4m3"):
    dtype, down = {"e4m3": (ml_dtypes.float8_e4m3fn, 7), "e5m2": (ml_dtypes.float8_e5m2, 14)}[fmt]
    v = np.moveaxis(np.asarray(x, np.float32).astype(ml_dtypes.bfloat16).astype(np.float64), axis, -1)
    blocks = v.reshape(v.shape[:-1] + (-1, 32))
    amax = np.abs(blocks).max(-1, keepdims=True)
    byte = np.maximum(np.where(amax > 0, np.frexp(amax)[1] - 1 + 127, 0) - down, 1)
    scale = np.exp2(byte - 127.0)
    codes = (blocks / scale).astype(np.float32).astype(dtype).astype(np.float64)
    return np.moveaxis((codes * scale).reshape(v.shape), -1, axis)


WIDE = False


def mx_kscale(k):
    if not WIDE:
        return np.ones(k)
    levels = np.array([10, -10, 5, -5, 0])
    if k % 512:
        return np.exp2(np.random.permutation(np.resize(levels, k // 32))).repeat(32)
    a = np.empty((k // 512, 16))
    for p in range(k // 512):
        a[p, :8] = np.random.permutation(np.resize(levels, 8))
        for g in range(8):
            far = levels[np.abs(levels - a[p, g]) >= 10]
            a[p, g + 8] = far[np.random.randint(len(far))]
    return np.exp2(a.ravel()).repeat(32)


def f64(x):
    return np.asarray(x).astype(np.float64)


def striped(idx):
    return np.tile(np.asarray(idx).reshape(-1, 16).T, (8, 1)).astype(np.uint16)


def unstriped(offs):
    return offs[:16].T.reshape(-1).astype(np.int64)


E2M1 = np.array([0.0, 0.5, 1.0, 1.5, 2.0, 3.0, 4.0, 6.0, -0.0, -0.5, -1.0, -1.5, -2.0, -3.0, -4.0, -6.0])


def pack_weight(w, fmt):
    k, n = w.shape
    w = f64(np.asarray(w, np.float32).astype(ml_dtypes.bfloat16)).reshape(k // 32, 32, n)
    amax = np.abs(w).max(1)
    if fmt == "e4m3":
        byte = np.frexp(amax)[1] - 1 + 127 - 7
    else:
        mant, ex = np.frexp(amax / 6.0)
        byte = np.where(mant > 0.5, ex, ex - 1) + 127
    byte = np.clip(np.where(amax > 0, byte, 1), 1, 254)
    scaled = (w * np.exp2(127.0 - byte)[:, None, :]).reshape(k, n).astype(np.float32)
    by_word = np.ascontiguousarray(scaled.reshape(k // 512, 128, 4, n).transpose(0, 1, 3, 2))
    if fmt == "e4m3":
        words = by_word.astype(ml_dtypes.float8_e4m3fn).view(np.uint8)
    else:
        c = by_word.astype(ml_dtypes.float4_e2m1fn).view(np.uint8) & 0xF
        words = (c[..., 0::2] | (c[..., 1::2] << 4)).reshape(k // 512, 128, 2 * n)
    return np.ascontiguousarray(words), np.ascontiguousarray(byte.astype(np.uint8).reshape(k // 512, 16, n))


def unpack_weight(words, scales, fmt):
    g, _, n = scales.shape
    words = np.ascontiguousarray(words).reshape(g, 128, n, -1)
    if fmt == "e4m3":
        vals = words.view(ml_dtypes.float8_e4m3fn).astype(np.float64)
    else:
        nib = np.empty((g, 128, n, 4), np.uint8)
        nib[..., 0::2] = words & 0xF
        nib[..., 1::2] = words >> 4
        vals = E2M1[nib]
    vals = vals * np.repeat(np.exp2(scales.astype(np.float64) - 127.0), 8, axis=1)[..., None]
    return vals.transpose(0, 1, 3, 2).reshape(g * 512, n)


K, T, J, L, I, M, N = 512, 2048, 1024, 512, 512, 512, 512


def setup_inputs():
    n = np.random.standard_normal
    idx = np.random.permutation(T)[:J]
    idx2 = np.random.permutation(J)[:I]
    fk = mx_kscale(K)
    fl = mx_kscale(L)
    fm = mx_kscale(M)
    xqp = pack_weight(n((K, T)) / fk[:, None], "e2m1")
    wap = pack_weight(n((K, N)) * 1 / np.sqrt(K) * fk[:, None], "e2m1")
    xbp = pack_weight(n((L, J)) / fl[:, None], "e4m3")
    wbp = pack_weight(n((L, N)) * 1 / np.sqrt(L) * fl[:, None], "e2m1")
    wcp = pack_weight(n((M, N)) * 1 / np.sqrt(M) * fm[:, None], "e4m3")
    return {
        "xq_words": xqp[0],
        "xq_scales": xqp[1],
        "wa_words": wap[0],
        "wa_scales": wap[1],
        "xb_words": xbp[0],
        "xb_scales": xbp[1],
        "wb_words": wbp[0],
        "wb_scales": wbp[1],
        "xc": (n((M, I)) / fm[:, None]).astype(np.float32),
        "wc_words": wcp[0],
        "wc_scales": wcp[1],
        "offs": striped(idx),
        "offs2": striped(idx2),
    }


def reference(xq_words, xq_scales, wa_words, wa_scales, xb_words, xb_scales, wb_words, wb_scales, xc, wc_words, wc_scales, offs, offs2):
    idx = unstriped(offs)
    idx2 = unstriped(offs2)
    xqu = unpack_weight(xq_words, xq_scales, "e2m1")
    wau = unpack_weight(wa_words, wa_scales, "e2m1")
    xbu = unpack_weight(xb_words, xb_scales, "e4m3")
    wbu = unpack_weight(wb_words, wb_scales, "e2m1")
    wcu = unpack_weight(wc_words, wc_scales, "e4m3")
    z = wau.T @ xqu
    p = wbu.T @ xbu
    xcq = mxq(f64(xc), 0, "e4m3")
    q = wcu.T @ xcq
    qs = np.zeros((N, J))
    qs[:, idx2] = q
    s = p + qs
    sp = np.zeros((N, T))
    sp[:, idx] = s
    y = z + sp
    return y

@@ -1,0 +1,240 @@
+from contextlib import ExitStack
+
+import concourse.mybir as mybir
+from concourse.masks import make_identity
+
+K, T, J, I, N = 512, 2048, 1024, 512, 512
+FLOPS = 2 * K * N * (T + J + I)
+
+F32 = mybir.dt.float32
+BF16 = mybir.dt.bfloat16
+I32 = mybir.dt.int32
+U32 = mybir.dt.uint32
+U16 = mybir.dt.uint16
+U8 = mybir.dt.uint8
+FP8X4 = mybir.dt.float8_e4m3fn_x4
+FP4X4 = mybir.dt.float4_e2m1fn_x4
+ADD = mybir.AluOpType.add
+
+P = 128
+PACK = 4
+BANK = 512
+ROW_TILES = N // P
+XC_CHUNKS = ((0, 128), (128, 256), (256, 512))
+CLEAR = 512
+
+
+def tile_list_three_tiers_nested_kernel(
+    tc, xq_words, xq_scales, wa_words, wa_scales, xb_words, xb_scales, wb_words, wb_scales,
+    xc, wc_words, wc_scales, offs, offs2, out,
+):
+    nc = tc.nc
+    with ExitStack() as ctx:
+        keep = ctx.enter_context(tc.tile_pool(name="keep", bufs=1))
+        ring = ctx.enter_context(tc.tile_pool(name="ring", bufs=4))
+        psum = ctx.enter_context(tc.psum_pool(name="psum", bufs=1))
+
+        def plane(name, width):
+            return keep.tile([P, width], U8, name=name, align_bytes=64)
+
+        def load_plane(queue, tile, rows):
+            for quad in range(4):
+                queue.dma_start(
+                    out=tile[32 * quad : 32 * quad + 4, :].bitcast(I32),
+                    in_=rows[0, 4 * quad : 4 * quad + 4, :].bitcast(I32),
+                )
+
+        def load_e4m3(name, words, width):
+            tile = keep.tile([P, width], U32, name=name, align_bytes=64)
+            nc.sync.dma_start(out=tile[:].bitcast(I32), in_=words[0].rearrange("p n t -> p (n t)").bitcast(I32))
+            return tile
+
+        def load_e2m1(name, words, width):
+            tile = keep.tile([P, 2 * width], U8, name=name, align_bytes=64)
+            nc.sync.dma_start(out=tile[:].bitcast(I32), in_=words[0].bitcast(I32))
+            return tile
+
+        wc_s, wb_s, xb_s = plane("wc_s", N), plane("wb_s", N), plane("xb_s", J)
+        wa_s, xq_s = plane("wa_s", N), plane("xq_s", T)
+        qs = [keep.tile([P, J], F32, name=f"qs{b}") for b in range(2)]
+
+        nc.vector.memset(wc_s[:].bitcast(U32), 0)
+        nc.vector.memset(qs[0][:], 0.0)
+        for tile in (wb_s, xb_s, wa_s, xq_s):
+            nc.vector.memset(tile[:].bitcast(U32), 0)
+        nc.vector.memset(qs[1][:], 0.0)
+
+        xc_rows = xc.rearrange("(p j) i -> p j i", j=PACK)
+        xc_raw = [keep.tile([P, PACK, hi - lo], F32, name=f"xc_raw{lo}") for lo, hi in XC_CHUNKS]
+
+        def load_xc(c):
+            lo, hi = XC_CHUNKS[c]
+            nc.sync.dma_start(out=xc_raw[c][:], in_=xc_rows[:, :, lo:hi])
+
+        load_xc(0)
+        load_plane(nc.scalar, wc_s, wc_scales)
+        wc_w = load_e4m3("wc_w", wc_words, N)
+        list2 = keep.tile([P, I // 16], U16, name="list2")
+        nc.sync.dma_start(list2[:], offs2)
+        load_xc(1)
+        load_xc(2)
+        wb_w = load_e2m1("wb_w", wb_words, N)
+        xb_w = load_e4m3("xb_w", xb_words, J)
+        load_plane(nc.sync, wb_s, wb_scales)
+        load_plane(nc.sync, xb_s, xb_scales)
+        list1 = keep.tile([P, J // 16], U16, name="list1")
+        nc.sync.dma_start(list1[:], offs)
+        wa_w = load_e2m1("wa_w", wa_words, N)
+        xq_w = load_e2m1("xq_w", xq_words, T)
+        load_plane(nc.sync, wa_s, wa_scales)
+        load_plane(nc.sync, xq_s, xq_scales)
+
+        ident = keep.tile([P, P], F32, name="ident")
+        make_identity(nc, ident[:])
+
+        xc_w = keep.tile([P, I], U32, name="xc_w", align_bytes=64)
+        xc_s = plane("xc_s", I)
+        xc_bf = [
+            keep.tile([P, hi - lo, PACK], BF16, name=f"xc_bf{lo}", tag=f"slot{c}", align_bytes=64)
+            for c, (lo, hi) in enumerate(XC_CHUNKS)
+        ]
+        taken = []
+
+        def bank_tile(b):
+            return psum.tile([P, BANK], F32, name=f"bank{b}", tag=f"bank{b}")[:]
+
+        def next_bank():
+            b = len(taken) % 8
+            taken.append(b)
+            return bank_tile(b)
+
+        q_sb = [keep.tile([P, I], F32, name=f"q_sb{r}") for r in range(ROW_TILES)]
+        p_sb = [keep.tile([P, J], F32, name=f"p_sb{r}") for r in range(ROW_TILES)]
+        zt_sb = [keep.tile([P, N], F32, name=f"zt_sb{j}") for j in range(T // P)]
+
+        def round_xc(c, copy):
+            copy(
+                out=xc_bf[c][:].rearrange("p (c i) t -> p c t i", i=4),
+                in_=xc_raw[c][:].rearrange("p t (c i) -> p c t i", i=4),
+            )
+
+        def quantise_xc(c):
+            lo, hi = XC_CHUNKS[c]
+            nc.vector.quantize_mx(
+                out=xc_w[:, lo:hi].bitcast(FP8X4), scales=xc_s[:, lo:hi], in_=xc_bf[c][:].rearrange("p i t -> p (i t)")
+            )
+
+        def q_product(dst, r, lo, hi):
+            rows = slice(P * r, P * (r + 1))
+            nc.tensor.matmul_mx(
+                out=dst, lhsT=wc_w[:, rows].bitcast(FP8X4), lhsT_scale=wc_s[:, rows],
+                rhs=xc_w[:, lo:hi].bitcast(FP8X4), rhs_scale=xc_s[:, lo:hi], start=True, stop=True,
+            )
+
+        def q_chunk(c):
+            lo, hi = XC_CHUNKS[c]
+            bank = next_bank()
+            for r in range(2):
+                q_product(bank[:, r * (hi - lo) : (r + 1) * (hi - lo)], r, lo, hi)
+            for r in range(2):
+                nc.scalar.copy(out=q_sb[r][:, lo:hi], in_=bank[:, r * (hi - lo) : (r + 1) * (hi - lo)])
+
+        def q_whole(r):
+            bank = next_bank()
+            q_product(bank, r, 0, I)
+            nc.scalar.copy(out=q_sb[r][:], in_=bank)
+
+        def scatter_q(r, lo, hi):
+            nc.vector.tensor_copy(qs[r % 2][:].indirect(list2[:, lo // 16 : hi // 16]), q_sb[r][:, lo:hi])
+
+        def e2m1_columns(tile, lo, hi):
+            return tile[:, 2 * lo : 2 * hi].bitcast(FP4X4)
+
+        def p_rows(r):
+            for lo in range(0, J, BANK):
+                bank = next_bank()
+                nc.tensor.matmul_mx(
+                    out=bank, lhsT=e2m1_columns(wb_w, P * r, P * (r + 1)), lhsT_scale=wb_s[:, P * r : P * (r + 1)],
+                    rhs=xb_w[:, lo : lo + BANK].bitcast(FP8X4), rhs_scale=xb_s[:, lo : lo + BANK], start=True, stop=True,
+                )
+                nc.scalar.copy(out=p_sb[r][:, lo : lo + BANK], in_=bank)
+
+        def z_tokens(j):
+            bank = next_bank()
+            nc.tensor.matmul_mx(
+                out=bank, lhsT=e2m1_columns(xq_w, P * j, P * (j + 1)), lhsT_scale=xq_s[:, P * j : P * (j + 1)],
+                rhs=e2m1_columns(wa_w, 0, N), rhs_scale=wa_s[:], start=True, stop=True,
+            )
+            nc.scalar.copy(out=zt_sb[j][:], in_=bank)
+
+        def scatter_s(r):
+            nc.vector.tensor_tensor(sp[r % 2][:].indirect(list1[:]), p_sb[r][:], qs[r % 2][:], ADD)
+
+        def turn(dst, src, start, stop):
+            nc.tensor.matmul(dst, src, ident[:], start=start, stop=stop, is_transpose=True)
+
+        def open_sums(r, close):
+            sums = [bank_tile(4 * ((r + 1) % 2) + b) for b in range(4)]
+            for j in range(T // P):
+                c = P * (j % 4)
+                turn(sums[j // 4][:, c : c + P], zt_sb[j][:, P * r : P * (r + 1)], j % 4 == 0, close and j % 4 == 3)
+            return sums
+
+        def add_by_transposes(r):
+            sums = open_sums(r, False)
+            turned = [bank_tile(4 * (r % 2) + b) for b in range(4)]
+            for j in range(T // P):
+                c = P * (j % 4)
+                nc.tensor.transpose(turned[j // 4][:, c : c + P], sp[r % 2][:, P * j : P * (j + 1)], ident[:])
+            turned_sb = [ring.tile([P, BANK], F32, name="turned_sb") for b in range(4)]
+            for b in range(4):
+                nc.scalar.copy(out=turned_sb[b][:], in_=turned[b])
+            for b in range(4):
+                for c in range(0, BANK, P):
+                    turn(sums[b][:, c : c + P], turned_sb[b][:, c : c + P], False, c == BANK - P)
+                y = ring.tile([P, BANK], F32, name="y")
+                nc.scalar.copy(out=y[:], in_=sums[b])
+                nc.sync.dma_start(out=out[P * r : P * (r + 1), BANK * b : BANK * (b + 1)], in_=y[:])
+
+        def add_on_vector(r):
+            sums = open_sums(r, True)
+            for b in range(4):
+                cols = slice(BANK * b, BANK * (b + 1))
+                y = ring.tile([P, BANK], F32, name="y_last")
+                nc.vector.tensor_tensor(y[:], sums[b], sp[r % 2][:, cols], ADD)
+                nc.sync.dma_start(out=out[P * r : P * (r + 1), cols], in_=y[:])
+
+        round_xc(0, nc.vector.tensor_copy)
+        quantise_xc(0)
+        q_chunk(0)
+        round_xc(1, nc.vector.tensor_copy)
+        quantise_xc(1)
+        q_chunk(1)
+        round_xc(2, nc.scalar.copy)
+        quantise_xc(2)
+        q_chunk(2)
+        for c in range(len(XC_CHUNKS)):
+            for r in range(2):
+                scatter_q(r, *XC_CHUNKS[c])
+        sp = [keep.tile([P, T], F32, name=f"sp{b}", tag=f"slot{b + 1}", align_bytes=64) for b in range(2)]
+        for tile in sp:
+            for lo in range(0, T, CLEAR):
+                nc.gpsimd.memset(tile[:, lo : lo + CLEAR], 0.0)
+        p_rows(0)
+        q_whole(2)
+        p_rows(1)
+        q_whole(3)
+        p_rows(2)
+        p_rows(3)
+        for j in range(T // P):
+            z_tokens(j)
+        scatter_s(0)
+        add_by_transposes(0)
+        scatter_q(2, 0, I)
+        scatter_s(1)
+        add_by_transposes(1)
+        scatter_q(3, 0, I)
+        scatter_s(2)
+        add_by_transposes(2)
+        scatter_s(3)
+        add_on_vector(3)

@@ -22,6 +22,8 @@ BANK = 512
 ROW_TILES = N // P
 XC_CHUNKS = ((0, 128), (128, 256), (256, 512))
 CLEAR = 512
+TAIL = (256, 256, 512, 512, 256, 256)
+QS_OF = (0, 1, 0, 0)
 
 
 def tile_list_three_tiers_nested_kernel(
@@ -58,14 +60,11 @@ def tile_list_three_tiers_nested_kernel(
         wa_s, xq_s = plane("wa_s", N), plane("xq_s", T)
         qs = [keep.tile([P, J], F32, name=f"qs{b}") for b in range(2)]
 
-        nc.vector.memset(wc_s[:].bitcast(U32), 0)
         nc.vector.memset(qs[0][:], 0.0)
-        for tile in (wb_s, xb_s, wa_s, xq_s):
-            nc.vector.memset(tile[:].bitcast(U32), 0)
         nc.vector.memset(qs[1][:], 0.0)
 
         xc_rows = xc.rearrange("(p j) i -> p j i", j=PACK)
-        xc_raw = [keep.tile([P, PACK, hi - lo], F32, name=f"xc_raw{lo}") for lo, hi in XC_CHUNKS]
+        xc_raw = [keep.tile([P, PACK, hi - lo], F32, name=f"xc_raw{lo}", tag=f"xc_raw{lo}") for lo, hi in XC_CHUNKS]
 
         def load_xc(c):
             lo, hi = XC_CHUNKS[c]
@@ -95,7 +94,7 @@ def tile_list_three_tiers_nested_kernel(
         xc_w = keep.tile([P, I], U32, name="xc_w", align_bytes=64)
         xc_s = plane("xc_s", I)
         xc_bf = [
-            keep.tile([P, hi - lo, PACK], BF16, name=f"xc_bf{lo}", tag=f"slot{c}", align_bytes=64)
+            keep.tile([P, hi - lo, PACK], BF16, name=f"xc_bf{lo}", align_bytes=64)
             for c, (lo, hi) in enumerate(XC_CHUNKS)
         ]
         taken = []
@@ -108,7 +107,7 @@ def tile_list_three_tiers_nested_kernel(
             taken.append(b)
             return bank_tile(b)
 
-        q_sb = [keep.tile([P, I], F32, name=f"q_sb{r}") for r in range(ROW_TILES)]
+        q_sb = {}
         p_sb = [keep.tile([P, J], F32, name=f"p_sb{r}") for r in range(ROW_TILES)]
         zt_sb = [keep.tile([P, N], F32, name=f"zt_sb{j}") for j in range(T // P)]
 
@@ -136,16 +135,21 @@ def tile_list_three_tiers_nested_kernel(
             bank = next_bank()
             for r in range(2):
                 q_product(bank[:, r * (hi - lo) : (r + 1) * (hi - lo)], r, lo, hi)
-            for r in range(2):
-                nc.scalar.copy(out=q_sb[r][:, lo:hi], in_=bank[:, r * (hi - lo) : (r + 1) * (hi - lo)])
+            return bank
+
+        def copy_q(bank, c, r, tag):
+            lo, hi = XC_CHUNKS[c]
+            q_sb[r, lo] = keep.tile([P, hi - lo], F32, name=f"q_sb{r}_{lo}", tag=tag)
+            nc.scalar.copy(out=q_sb[r, lo][:], in_=bank[:, r * (hi - lo) : (r + 1) * (hi - lo)])
 
         def q_whole(r):
             bank = next_bank()
             q_product(bank, r, 0, I)
-            nc.scalar.copy(out=q_sb[r][:], in_=bank)
+            q_sb[r, 0] = keep.tile([P, I], F32, name=f"q_sb{r}")
+            nc.scalar.copy(out=q_sb[r, 0][:], in_=bank)
 
         def scatter_q(r, lo, hi):
-            nc.vector.tensor_copy(qs[r % 2][:].indirect(list2[:, lo // 16 : hi // 16]), q_sb[r][:, lo:hi])
+            nc.vector.tensor_copy(qs[QS_OF[r]][:].indirect(list2[:, lo // 16 : hi // 16]), q_sb[r, lo][:])
 
         def e2m1_columns(tile, lo, hi):
             return tile[:, 2 * lo : 2 * hi].bitcast(FP4X4)
@@ -168,7 +172,7 @@ def tile_list_three_tiers_nested_kernel(
             nc.scalar.copy(out=zt_sb[j][:], in_=bank)
 
         def scatter_s(r):
-            nc.vector.tensor_tensor(sp[r % 2][:].indirect(list1[:]), p_sb[r][:], qs[r % 2][:], ADD)
+            nc.vector.tensor_tensor(sp[r % 2][:].indirect(list1[:]), p_sb[r][:], qs[QS_OF[r]][:], ADD)
 
         def turn(dst, src, start, stop):
             nc.tensor.matmul(dst, src, ident[:], start=start, stop=stop, is_transpose=True)
@@ -198,28 +202,36 @@ def tile_list_three_tiers_nested_kernel(
 
         def add_on_vector(r):
             sums = open_sums(r, True)
-            for b in range(4):
-                cols = slice(BANK * b, BANK * (b + 1))
-                y = ring.tile([P, BANK], F32, name="y_last")
-                nc.vector.tensor_tensor(y[:], sums[b], sp[r % 2][:, cols], ADD)
-                nc.sync.dma_start(out=out[P * r : P * (r + 1), cols], in_=y[:])
+            lo = 0
+            for width in TAIL:
+                b, c = divmod(lo, BANK)
+                y = keep.tile([P, width], F32, name=f"y_last{lo}")
+                nc.vector.tensor_tensor(y[:], sums[b][:, c : c + width], sp[r % 2][:, lo : lo + width], ADD)
+                nc.sync.dma_start(out=out[P * r : P * (r + 1), lo : lo + width], in_=y[:])
+                lo += width
 
         round_xc(0, nc.vector.tensor_copy)
         quantise_xc(0)
-        q_chunk(0)
+        bank = q_chunk(0)
+        copy_q(bank, 0, 0, "q00")
+        copy_q(bank, 0, 1, "q01")
         round_xc(1, nc.vector.tensor_copy)
         quantise_xc(1)
-        q_chunk(1)
+        bank = q_chunk(1)
+        copy_q(bank, 1, 0, "q10")
         round_xc(2, nc.scalar.copy)
+        copy_q(bank, 1, 1, "xc_raw256")
         quantise_xc(2)
-        q_chunk(2)
+        bank = q_chunk(2)
+        copy_q(bank, 2, 0, "q20")
+        copy_q(bank, 2, 1, "q21")
         for c in range(len(XC_CHUNKS)):
             for r in range(2):
                 scatter_q(r, *XC_CHUNKS[c])
-        sp = [keep.tile([P, T], F32, name=f"sp{b}", tag=f"slot{b + 1}", align_bytes=64) for b in range(2)]
-        for tile in sp:
-            for lo in range(0, T, CLEAR):
-                nc.gpsimd.memset(tile[:, lo : lo + CLEAR], 0.0)
+        sp = [keep.tile([P, T], F32, name="sp0"), keep.tile([P, T], F32, name="sp1", tag="q21")]
+        for lo in range(0, T, CLEAR):
+            nc.vector.memset(sp[0][:, lo : lo + CLEAR], 0.0)
+        nc.gpsimd.memset(sp[1][:], 0.0)
         p_rows(0)
         q_whole(2)
         p_rows(1)
@@ -233,8 +245,8 @@ def tile_list_three_tiers_nested_kernel(
         scatter_q(2, 0, I)
         scatter_s(1)
         add_by_transposes(1)
-        scatter_q(3, 0, I)
         scatter_s(2)
         add_by_transposes(2)
+        scatter_q(3, 0, I)
         scatter_s(3)
         add_on_vector(3)

@@ -23,7 +23,7 @@ ROW_TILES = N // P
 XC_CHUNKS = ((0, 128), (128, 256), (256, 512))
 CLEAR = 512
 TAIL = (256, 256, 512, 512, 256, 256)
-QS_OF = (0, 1, 0, 0)
+QS_OF = (0, 1, 0, 1)
 
 
 def tile_list_three_tiers_nested_kernel(
@@ -88,28 +88,18 @@ def tile_list_three_tiers_nested_kernel(
         load_plane(nc.sync, wa_s, wa_scales)
         load_plane(nc.sync, xq_s, xq_scales)
 
-        ident = keep.tile([P, P], F32, name="ident")
-        make_identity(nc, ident[:])
-
         xc_w = keep.tile([P, I], U32, name="xc_w", align_bytes=64)
         xc_s = plane("xc_s", I)
         xc_bf = [
             keep.tile([P, hi - lo, PACK], BF16, name=f"xc_bf{lo}", align_bytes=64)
             for c, (lo, hi) in enumerate(XC_CHUNKS)
         ]
-        taken = []
-
         def bank_tile(b):
             return psum.tile([P, BANK], F32, name=f"bank{b}", tag=f"bank{b}")[:]
 
-        def next_bank():
-            b = len(taken) % 8
-            taken.append(b)
-            return bank_tile(b)
-
         q_sb = {}
         p_sb = [keep.tile([P, J], F32, name=f"p_sb{r}") for r in range(ROW_TILES)]
-        zt_sb = [keep.tile([P, N], F32, name=f"zt_sb{j}") for j in range(T // P)]
+        z_sb = [[keep.tile([P, BANK], F32, name=f"z_sb{r}_{k}") for k in range(4)] for r in range(ROW_TILES - 1)]
 
         def round_xc(c, copy):
             copy(
@@ -132,7 +122,7 @@ def tile_list_three_tiers_nested_kernel(
 
         def q_chunk(c):
             lo, hi = XC_CHUNKS[c]
-            bank = next_bank()
+            bank = bank_tile(c)
             for r in range(2):
                 q_product(bank[:, r * (hi - lo) : (r + 1) * (hi - lo)], r, lo, hi)
             return bank
@@ -142,8 +132,8 @@ def tile_list_three_tiers_nested_kernel(
             q_sb[r, lo] = keep.tile([P, hi - lo], F32, name=f"q_sb{r}_{lo}", tag=tag)
             nc.scalar.copy(out=q_sb[r, lo][:], in_=bank[:, r * (hi - lo) : (r + 1) * (hi - lo)])
 
-        def q_whole(r):
-            bank = next_bank()
+        def q_whole(r, b):
+            bank = bank_tile(b)
             q_product(bank, r, 0, I)
             q_sb[r, 0] = keep.tile([P, I], F32, name=f"q_sb{r}")
             nc.scalar.copy(out=q_sb[r, 0][:], in_=bank)
@@ -154,22 +144,28 @@ def tile_list_three_tiers_nested_kernel(
         def e2m1_columns(tile, lo, hi):
             return tile[:, 2 * lo : 2 * hi].bitcast(FP4X4)
 
-        def p_rows(r):
-            for lo in range(0, J, BANK):
-                bank = next_bank()
+        def p_rows(r, banks):
+            for lo, b in zip(range(0, J, BANK), banks):
+                bank = bank_tile(b)
                 nc.tensor.matmul_mx(
                     out=bank, lhsT=e2m1_columns(wb_w, P * r, P * (r + 1)), lhsT_scale=wb_s[:, P * r : P * (r + 1)],
                     rhs=xb_w[:, lo : lo + BANK].bitcast(FP8X4), rhs_scale=xb_s[:, lo : lo + BANK], start=True, stop=True,
                 )
                 nc.scalar.copy(out=p_sb[r][:, lo : lo + BANK], in_=bank)
 
-        def z_tokens(j):
-            bank = next_bank()
-            nc.tensor.matmul_mx(
-                out=bank, lhsT=e2m1_columns(xq_w, P * j, P * (j + 1)), lhsT_scale=xq_s[:, P * j : P * (j + 1)],
-                rhs=e2m1_columns(wa_w, 0, N), rhs_scale=wa_s[:], start=True, stop=True,
-            )
-            nc.scalar.copy(out=zt_sb[j][:], in_=bank)
+        def z_products(r):
+            banks = [bank_tile(k) for k in range(4)]
+            for k in range(4):
+                lo = BANK * k
+                nc.tensor.matmul_mx(
+                    out=banks[k], lhsT=e2m1_columns(wa_w, P * r, P * (r + 1)), lhsT_scale=wa_s[:, P * r : P * (r + 1)],
+                    rhs=e2m1_columns(xq_w, lo, lo + BANK), rhs_scale=xq_s[:, lo : lo + BANK], start=True, stop=True,
+                )
+            return banks
+
+        def z_rows(r):
+            for k, bank in enumerate(z_products(r)):
+                nc.scalar.copy(out=z_sb[r][k][:], in_=bank)
 
         def scatter_s(r):
             nc.vector.tensor_tensor(sp[r % 2][:].indirect(list1[:]), p_sb[r][:], qs[QS_OF[r]][:], ADD)
@@ -177,31 +173,29 @@ def tile_list_three_tiers_nested_kernel(
         def turn(dst, src, start, stop):
             nc.tensor.matmul(dst, src, ident[:], start=start, stop=stop, is_transpose=True)
 
-        def open_sums(r, close):
-            sums = [bank_tile(4 * ((r + 1) % 2) + b) for b in range(4)]
-            for j in range(T // P):
-                c = P * (j % 4)
-                turn(sums[j // 4][:, c : c + P], zt_sb[j][:, P * r : P * (r + 1)], j % 4 == 0, close and j % 4 == 3)
-            return sums
-
         def add_by_transposes(r):
-            sums = open_sums(r, False)
-            turned = [bank_tile(4 * (r % 2) + b) for b in range(4)]
-            for j in range(T // P):
-                c = P * (j % 4)
-                nc.tensor.transpose(turned[j // 4][:, c : c + P], sp[r % 2][:, P * j : P * (j + 1)], ident[:])
+            turned = [bank_tile(b) for b in range(4)]
+            for k in range(4):
+                for b in range(4):
+                    turn(turned[b][:, P * k : P * (k + 1)], z_sb[r][k][:, P * b : P * (b + 1)], k == 0, False)
+            for b in range(4):
+                for k in range(4):
+                    lo = BANK * k + P * b
+                    turn(turned[b][:, P * k : P * (k + 1)], sp[r % 2][:, lo : lo + P], False, k == 3)
             turned_sb = [ring.tile([P, BANK], F32, name="turned_sb") for b in range(4)]
             for b in range(4):
                 nc.scalar.copy(out=turned_sb[b][:], in_=turned[b])
+            out_blocks = out[P * r : P * (r + 1), :].rearrange("p (k b c) -> p b k c", k=4, b=4)
             for b in range(4):
+                back = bank_tile(4 + b)
                 for c in range(0, BANK, P):
-                    turn(sums[b][:, c : c + P], turned_sb[b][:, c : c + P], False, c == BANK - P)
+                    nc.tensor.transpose(back[:, c : c + P], turned_sb[b][:, c : c + P], ident[:])
                 y = ring.tile([P, BANK], F32, name="y")
-                nc.scalar.copy(out=y[:], in_=sums[b])
-                nc.sync.dma_start(out=out[P * r : P * (r + 1), BANK * b : BANK * (b + 1)], in_=y[:])
+                nc.scalar.copy(out=y[:], in_=back)
+                nc.sync.dma_start(out=out_blocks[:, b], in_=y[:].rearrange("p (k c) -> p k c", k=4))
 
         def add_on_vector(r):
-            sums = open_sums(r, True)
+            sums = z_products(r)
             lo = 0
             for width in TAIL:
                 b, c = divmod(lo, BANK)
@@ -228,25 +222,28 @@ def tile_list_three_tiers_nested_kernel(
         for c in range(len(XC_CHUNKS)):
             for r in range(2):
                 scatter_q(r, *XC_CHUNKS[c])
+        ident = keep.tile([P, P], F32, name="ident", tag="q00")
+        make_identity(nc, ident[:])
         sp = [keep.tile([P, T], F32, name="sp0"), keep.tile([P, T], F32, name="sp1", tag="q21")]
         for lo in range(0, T, CLEAR):
             nc.vector.memset(sp[0][:, lo : lo + CLEAR], 0.0)
         nc.gpsimd.memset(sp[1][:], 0.0)
-        p_rows(0)
-        q_whole(2)
-        p_rows(1)
-        q_whole(3)
-        p_rows(2)
-        p_rows(3)
-        for j in range(T // P):
-            z_tokens(j)
+        p_rows(0, (3, 4))
+        q_whole(2, 5)
+        p_rows(1, (6, 7))
+        z_rows(0)
+        q_whole(3, 4)
+        p_rows(2, (5, 6))
+        p_rows(3, (7, 4))
         scatter_s(0)
         add_by_transposes(0)
+        z_rows(1)
         scatter_q(2, 0, I)
         scatter_s(1)
         add_by_transposes(1)
+        z_rows(2)
+        scatter_q(3, 0, I)
         scatter_s(2)
         add_by_transposes(2)
-        scatter_q(3, 0, I)
         scatter_s(3)
         add_on_vector(3)

from contextlib import ExitStack

import concourse.mybir as mybir
from concourse.masks import make_identity

K, T, J, I, N = 512, 2048, 1024, 512, 512
FLOPS = 2 * K * N * (T + J + I)

F32 = mybir.dt.float32
BF16 = mybir.dt.bfloat16
I32 = mybir.dt.int32
U32 = mybir.dt.uint32
U16 = mybir.dt.uint16
U8 = mybir.dt.uint8
FP8X4 = mybir.dt.float8_e4m3fn_x4
FP4X4 = mybir.dt.float4_e2m1fn_x4
ADD = mybir.AluOpType.add

P = 128
PACK = 4
BANK = 512
ROW_TILES = N // P
XC_CHUNKS = ((0, 128), (128, 256), (256, 512))
CLEAR = 512
TAIL = (256, 256, 512, 512, 256, 256)
QS_OF = (0, 1, 0, 1)


def tile_list_three_tiers_nested_kernel(
    tc, xq_words, xq_scales, wa_words, wa_scales, xb_words, xb_scales, wb_words, wb_scales,
    xc, wc_words, wc_scales, offs, offs2, out,
):
    nc = tc.nc
    with ExitStack() as ctx:
        keep = ctx.enter_context(tc.tile_pool(name="keep", bufs=1))
        ring = ctx.enter_context(tc.tile_pool(name="ring", bufs=4))
        psum = ctx.enter_context(tc.psum_pool(name="psum", bufs=1))

        def plane(name, width):
            return keep.tile([P, width], U8, name=name, align_bytes=64)

        def load_plane(queue, tile, rows):
            for quad in range(4):
                queue.dma_start(
                    out=tile[32 * quad : 32 * quad + 4, :].bitcast(I32),
                    in_=rows[0, 4 * quad : 4 * quad + 4, :].bitcast(I32),
                )

        def load_e4m3(name, words, width):
            tile = keep.tile([P, width], U32, name=name, align_bytes=64)
            nc.sync.dma_start(out=tile[:].bitcast(I32), in_=words[0].rearrange("p n t -> p (n t)").bitcast(I32))
            return tile

        def load_e2m1(name, words, width):
            tile = keep.tile([P, 2 * width], U8, name=name, align_bytes=64)
            nc.sync.dma_start(out=tile[:].bitcast(I32), in_=words[0].bitcast(I32))
            return tile

        wc_s, wb_s, xb_s = plane("wc_s", N), plane("wb_s", N), plane("xb_s", J)
        wa_s, xq_s = plane("wa_s", N), plane("xq_s", T)
        qs = [keep.tile([P, J], F32, name=f"qs{b}") for b in range(2)]

        nc.vector.memset(qs[0][:], 0.0)
        nc.vector.memset(qs[1][:], 0.0)

        xc_rows = xc.rearrange("(p j) i -> p j i", j=PACK)
        xc_raw = [keep.tile([P, PACK, hi - lo], F32, name=f"xc_raw{lo}", tag=f"xc_raw{lo}") for lo, hi in XC_CHUNKS]

        def load_xc(c):
            lo, hi = XC_CHUNKS[c]
            nc.sync.dma_start(out=xc_raw[c][:], in_=xc_rows[:, :, lo:hi])

        load_xc(0)
        load_plane(nc.scalar, wc_s, wc_scales)
        wc_w = load_e4m3("wc_w", wc_words, N)
        list2 = keep.tile([P, I // 16], U16, name="list2")
        nc.sync.dma_start(list2[:], offs2)
        load_xc(1)
        load_xc(2)
        wb_w = load_e2m1("wb_w", wb_words, N)
        xb_w = load_e4m3("xb_w", xb_words, J)
        load_plane(nc.sync, wb_s, wb_scales)
        load_plane(nc.sync, xb_s, xb_scales)
        list1 = keep.tile([P, J // 16], U16, name="list1")
        nc.sync.dma_start(list1[:], offs)
        wa_w = load_e2m1("wa_w", wa_words, N)
        xq_w = load_e2m1("xq_w", xq_words, T)
        load_plane(nc.sync, wa_s, wa_scales)
        load_plane(nc.sync, xq_s, xq_scales)

        xc_w = keep.tile([P, I], U32, name="xc_w", align_bytes=64)
        xc_s = plane("xc_s", I)
        xc_bf = [
            keep.tile([P, hi - lo, PACK], BF16, name=f"xc_bf{lo}", align_bytes=64)
            for c, (lo, hi) in enumerate(XC_CHUNKS)
        ]
        def bank_tile(b):
            return psum.tile([P, BANK], F32, name=f"bank{b}", tag=f"bank{b}")[:]

        q_sb = {}
        p_sb = [keep.tile([P, J], F32, name=f"p_sb{r}") for r in range(ROW_TILES)]
        z_sb = [[keep.tile([P, BANK], F32, name=f"z_sb{r}_{k}") for k in range(4)] for r in range(ROW_TILES - 1)]

        def round_xc(c, copy):
            copy(
                out=xc_bf[c][:].rearrange("p (c i) t -> p c t i", i=4),
                in_=xc_raw[c][:].rearrange("p t (c i) -> p c t i", i=4),
            )

        def quantise_xc(c):
            lo, hi = XC_CHUNKS[c]
            nc.vector.quantize_mx(
                out=xc_w[:, lo:hi].bitcast(FP8X4), scales=xc_s[:, lo:hi], in_=xc_bf[c][:].rearrange("p i t -> p (i t)")
            )

        def q_product(dst, r, lo, hi):
            rows = slice(P * r, P * (r + 1))
            nc.tensor.matmul_mx(
                out=dst, lhsT=wc_w[:, rows].bitcast(FP8X4), lhsT_scale=wc_s[:, rows],
                rhs=xc_w[:, lo:hi].bitcast(FP8X4), rhs_scale=xc_s[:, lo:hi], start=True, stop=True,
            )

        def q_chunk(c):
            lo, hi = XC_CHUNKS[c]
            bank = bank_tile(c)
            for r in range(2):
                q_product(bank[:, r * (hi - lo) : (r + 1) * (hi - lo)], r, lo, hi)
            return bank

        def copy_q(bank, c, r, tag):
            lo, hi = XC_CHUNKS[c]
            q_sb[r, lo] = keep.tile([P, hi - lo], F32, name=f"q_sb{r}_{lo}", tag=tag)
            nc.scalar.copy(out=q_sb[r, lo][:], in_=bank[:, r * (hi - lo) : (r + 1) * (hi - lo)])

        def q_whole(r, b):
            bank = bank_tile(b)
            q_product(bank, r, 0, I)
            q_sb[r, 0] = keep.tile([P, I], F32, name=f"q_sb{r}")
            nc.scalar.copy(out=q_sb[r, 0][:], in_=bank)

        def scatter_q(r, lo, hi):
            nc.vector.tensor_copy(qs[QS_OF[r]][:].indirect(list2[:, lo // 16 : hi // 16]), q_sb[r, lo][:])

        def e2m1_columns(tile, lo, hi):
            return tile[:, 2 * lo : 2 * hi].bitcast(FP4X4)

        def p_rows(r, banks):
            for lo, b in zip(range(0, J, BANK), banks):
                bank = bank_tile(b)
                nc.tensor.matmul_mx(
                    out=bank, lhsT=e2m1_columns(wb_w, P * r, P * (r + 1)), lhsT_scale=wb_s[:, P * r : P * (r + 1)],
                    rhs=xb_w[:, lo : lo + BANK].bitcast(FP8X4), rhs_scale=xb_s[:, lo : lo + BANK], start=True, stop=True,
                )
                nc.scalar.copy(out=p_sb[r][:, lo : lo + BANK], in_=bank)

        def z_products(r):
            banks = [bank_tile(k) for k in range(4)]
            for k in range(4):
                lo = BANK * k
                nc.tensor.matmul_mx(
                    out=banks[k], lhsT=e2m1_columns(wa_w, P * r, P * (r + 1)), lhsT_scale=wa_s[:, P * r : P * (r + 1)],
                    rhs=e2m1_columns(xq_w, lo, lo + BANK), rhs_scale=xq_s[:, lo : lo + BANK], start=True, stop=True,
                )
            return banks

        def z_rows(r):
            for k, bank in enumerate(z_products(r)):
                nc.scalar.copy(out=z_sb[r][k][:], in_=bank)

        def scatter_s(r):
            nc.vector.tensor_tensor(sp[r % 2][:].indirect(list1[:]), p_sb[r][:], qs[QS_OF[r]][:], ADD)

        def turn(dst, src, start, stop):
            nc.tensor.matmul(dst, src, ident[:], start=start, stop=stop, is_transpose=True)

        def add_by_transposes(r):
            turned = [bank_tile(b) for b in range(4)]
            for k in range(4):
                for b in range(4):
                    turn(turned[b][:, P * k : P * (k + 1)], z_sb[r][k][:, P * b : P * (b + 1)], k == 0, False)
            for b in range(4):
                for k in range(4):
                    lo = BANK * k + P * b
                    turn(turned[b][:, P * k : P * (k + 1)], sp[r % 2][:, lo : lo + P], False, k == 3)
            turned_sb = [ring.tile([P, BANK], F32, name="turned_sb") for b in range(4)]
            for b in range(4):
                nc.scalar.copy(out=turned_sb[b][:], in_=turned[b])
            out_blocks = out[P * r : P * (r + 1), :].rearrange("p (k b c) -> p b k c", k=4, b=4)
            for b in range(4):
                back = bank_tile(4 + b)
                for c in range(0, BANK, P):
                    nc.tensor.transpose(back[:, c : c + P], turned_sb[b][:, c : c + P], ident[:])
                y = ring.tile([P, BANK], F32, name="y")
                nc.scalar.copy(out=y[:], in_=back)
                nc.sync.dma_start(out=out_blocks[:, b], in_=y[:].rearrange("p (k c) -> p k c", k=4))

        def add_on_vector(r):
            sums = z_products(r)
            lo = 0
            for width in TAIL:
                b, c = divmod(lo, BANK)
                y = keep.tile([P, width], F32, name=f"y_last{lo}")
                nc.vector.tensor_tensor(y[:], sums[b][:, c : c + width], sp[r % 2][:, lo : lo + width], ADD)
                nc.sync.dma_start(out=out[P * r : P * (r + 1), lo : lo + width], in_=y[:])
                lo += width

        round_xc(0, nc.vector.tensor_copy)
        quantise_xc(0)
        bank = q_chunk(0)
        copy_q(bank, 0, 0, "q00")
        copy_q(bank, 0, 1, "q01")
        round_xc(1, nc.vector.tensor_copy)
        quantise_xc(1)
        bank = q_chunk(1)
        copy_q(bank, 1, 0, "q10")
        round_xc(2, nc.scalar.copy)
        copy_q(bank, 1, 1, "xc_raw256")
        quantise_xc(2)
        bank = q_chunk(2)
        copy_q(bank, 2, 0, "q20")
        copy_q(bank, 2, 1, "q21")
        for c in range(len(XC_CHUNKS)):
            for r in range(2):
                scatter_q(r, *XC_CHUNKS[c])
        ident = keep.tile([P, P], F32, name="ident", tag="q00")
        make_identity(nc, ident[:])
        sp = [keep.tile([P, T], F32, name="sp0"), keep.tile([P, T], F32, name="sp1", tag="q21")]
        for lo in range(0, T, CLEAR):
            nc.vector.memset(sp[0][:, lo : lo + CLEAR], 0.0)
        nc.gpsimd.memset(sp[1][:], 0.0)
        p_rows(0, (3, 4))
        q_whole(2, 5)
        p_rows(1, (6, 7))
        z_rows(0)
        q_whole(3, 4)
        p_rows(2, (5, 6))
        p_rows(3, (7, 4))
        scatter_s(0)
        add_by_transposes(0)
        z_rows(1)
        scatter_q(2, 0, I)
        scatter_s(1)
        add_by_transposes(1)
        z_rows(2)
        scatter_q(3, 0, I)
        scatter_s(2)
        add_by_transposes(2)
        scatter_s(3)
        add_on_vector(3)
